import numpy as np
import ml_dtypes


def mxq(x, axis, fmt="e4m3"):
    dtype, down = {"e4m3": (ml_dtypes.float8_e4m3fn, 7), "e5m2": (ml_dtypes.float8_e5m2, 14)}[fmt]
    v = np.moveaxis(np.asarray(x, np.float32).astype(ml_dtypes.bfloat16).astype(np.float64), axis, -1)
    blocks = v.reshape(v.shape[:-1] + (-1, 32))
    amax = np.abs(blocks).max(-1, keepdims=True)
    byte = np.maximum(np.where(amax > 0, np.frexp(amax)[1] - 1 + 127, 0) - down, 1)
    scale = np.exp2(byte - 127.0)
    codes = (blocks / scale).astype(np.float32).astype(dtype).astype(np.float64)
    return np.moveaxis((codes * scale).reshape(v.shape), -1, axis)


WIDE = False


def mx_kscale(k):
    if not WIDE:
        return np.ones(k)
    levels = np.array([10, -10, 5, -5, 0])
    if k % 512:
        return np.exp2(np.random.permutation(np.resize(levels, k // 32))).repeat(32)
    a = np.empty((k // 512, 16))
    for p in range(k // 512):
        a[p, :8] = np.random.permutation(np.resize(levels, 8))
        for g in range(8):
            far = levels[np.abs(levels - a[p, g]) >= 10]
            a[p, g + 8] = far[np.random.randint(len(far))]
    return np.exp2(a.ravel()).repeat(32)


def f64(x):
    return np.asarray(x).astype(np.float64)


def striped8(idx):
    return np.asarray(idx).reshape(8, -1, 16).transpose(0, 2, 1).reshape(128, -1).astype(np.uint16)


def unstriped8(offs):
    return offs.reshape(8, 16, -1).transpose(0, 2, 1).reshape(8, -1).astype(np.int64)


def pick8(x, idx, run):
    r = np.arange(len(x))
    return x[r[:, None], idx[r % (8 * run) // run]]


E2M1 = np.array([0.0, 0.5, 1.0, 1.5, 2.0, 3.0, 4.0, 6.0, -0.0, -0.5, -1.0, -1.5, -2.0, -3.0, -4.0, -6.0])


def pack_weight(w, fmt):
    k, n = w.shape
    w = f64(np.asarray(w, np.float32).astype(ml_dtypes.bfloat16)).reshape(k // 32, 32, n)
    amax = np.abs(w).max(1)
    if fmt == "e4m3":
        byte = np.frexp(amax)[1] - 1 + 127 - 7
    else:
        mant, ex = np.frexp(amax / 6.0)
        byte = np.where(mant > 0.5, ex, ex - 1) + 127
    byte = np.clip(np.where(amax > 0, byte, 1), 1, 254)
    scaled = (w * np.exp2(127.0 - byte)[:, None, :]).reshape(k, n).astype(np.float32)
    by_word = np.ascontiguousarray(scaled.reshape(k // 512, 128, 4, n).transpose(0, 1, 3, 2))
    if fmt == "e4m3":
        words = by_word.astype(ml_dtypes.float8_e4m3fn).view(np.uint8)
    else:
        c = by_word.astype(ml_dtypes.float4_e2m1fn).view(np.uint8) & 0xF
        words = (c[..., 0::2] | (c[..., 1::2] << 4)).reshape(k // 512, 128, 2 * n)
    return np.ascontiguousarray(words), np.ascontiguousarray(byte.astype(np.uint8).reshape(k // 512, 16, n))


def unpack_weight(words, scales, fmt):
    g, _, n = scales.shape
    words = np.ascontiguousarray(words).reshape(g, 128, n, -1)
    if fmt == "e4m3":
        vals = words.view(ml_dtypes.float8_e4m3fn).astype(np.float64)
    else:
        nib = np.empty((g, 128, n, 4), np.uint8)
        nib[..., 0::2] = words & 0xF
        nib[..., 1::2] = words >> 4
        vals = E2M1[nib]
    vals = vals * np.repeat(np.exp2(scales.astype(np.float64) - 127.0), 8, axis=1)[..., None]
    return vals.transpose(0, 1, 3, 2).reshape(g * 512, n)


D, T, U, I, Q = 512, 1024, 1024, 512, 128


def setup_inputs():
    n = np.random.standard_normal
    idx = np.stack([np.random.permutation(T)[:I] for _ in range(8)])
    idx2 = np.stack([np.random.permutation(U)[:I] for _ in range(8)])
    idx3 = np.stack([np.random.permutation(U)[:I] for _ in range(8)])
    idx4 = np.stack([np.random.permutation(T)[:I] for _ in range(8)])
    idx5 = np.stack([np.random.permutation(U)[:I] for _ in range(8)])
    fd = mx_kscale(D)
    cachep = pack_weight(n((D, T)) / fd[:, None], "e2m1")
    draftp = pack_weight(n((D, U)) / fd[:, None], "e4m3")
    return {
        "query": (n((D, Q)) * 1.0 / np.sqrt(D) * fd[:, None]).astype(np.float32),
        "cache_words": cachep[0],
        "cache_scales": cachep[1],
        "draft_words": draftp[0],
        "draft_scales": draftp[1],
        "offs": striped8(idx),
        "offs2": striped8(idx2),
        "offs3": striped8(idx3),
        "offs4": striped8(idx4),
        "offs5": striped8(idx5),
    }


def reference(query, cache_words, cache_scales, draft_words, draft_scales, offs, offs2, offs3, offs4, offs5):
    idx = unstriped8(offs)
    idx2 = unstriped8(offs2)
    idx3 = unstriped8(offs3)
    idx4 = unstriped8(offs4)
    idx5 = unstriped8(offs5)
    cacheu = unpack_weight(cache_words, cache_scales, "e2m1")
    draftu = unpack_weight(draft_words, draft_scales, "e4m3")
    queryq = mxq(f64(query), 0, "e4m3")
    a = queryq.T @ cacheu
    b = queryq.T @ draftu
    w = np.maximum(pick8(a, idx, 16), pick8(b, idx2, 16))
    mu = np.mean(w, axis=1, keepdims=True)
    v = w - mu
    f1 = np.zeros((Q, U))
    f1[np.arange(Q)[:, None], idx3[np.arange(Q) % 128 // 16]] = v
    f2 = np.zeros((Q, T))
    f2[np.arange(Q)[:, None], idx4[np.arange(Q) % 128 // 16]] = v
    bb = b - f1
    aa = a + f2
    r = pick8(bb, idx5, 16) + pick8(aa, idx, 16)
    y = np.minimum(r, w)
    return y

@@ -1,0 +1,127 @@
+from contextlib import ExitStack
+
+import concourse.mybir as mybir
+
+F32 = mybir.dt.float32
+BF16 = mybir.dt.bfloat16
+I32 = mybir.dt.int32
+U32 = mybir.dt.uint32
+U16 = mybir.dt.uint16
+U8 = mybir.dt.uint8
+FP8X4 = mybir.dt.float8_e4m3fn_x4
+FP4X4 = mybir.dt.float4_e2m1fn_x4
+ALU = mybir.AluOpType
+COPY = mybir.ActivationFunctionType.Copy
+
+P = 128
+D, T, SLOTS, Q = 512, 1024, 512, 128
+PACK = 4
+CHUNK = 256
+HALF = SLOTS // 2
+LIST_COLS = SLOTS // 16
+DRAFT_ROW = 4
+
+FLOPS = 2 * D * Q * 2 * T
+
+
+def tile_attend_centredwrites_two_kernel(tc, query, cache_words, cache_scales, draft_words, draft_scales,
+                                          offs, offs2, offs3, offs4, offs5, out):
+    nc = tc.nc
+    with ExitStack() as ctx:
+        held = ctx.enter_context(tc.tile_pool(name="held", bufs=1))
+        psum = ctx.enter_context(tc.psum_pool(name="psum", bufs=1))
+
+        cache_plane = held.tile([P, 2 * T], U8, align_bytes=64)
+        draft_plane = held.tile([P, 2 * T], U8, align_bytes=64)
+        nc.vector.memset(cache_plane[0:64, :].bitcast(I32), 0)
+        nc.vector.memset(draft_plane[64:128, :].bitcast(I32), 0)
+
+        q_raw = held.tile([P, PACK, Q], F32)
+        nc.sync.dma_start(q_raw[:], query.rearrange("(p j) w -> p j w", j=PACK))
+
+        cache_rows = cache_scales[0].bitcast(I32).rearrange("(h q k) n -> q k h n", h=2, q=2)
+        draft_rows = draft_scales[0].bitcast(I32).rearrange("(h q k) n -> q k h n", h=2, q=2)
+        for q in range(2):
+            nc.scalar.dma_start(cache_plane[32 * q : 32 * q + 4, :].bitcast(I32).rearrange("p (h n) -> p h n", h=2), cache_rows[q])
+        cache_codes = held.tile([P, 2 * T], U8, align_bytes=64)
+        nc.sync.dma_start(cache_codes[:].bitcast(I32), cache_words[0].bitcast(I32))
+        for q in range(2):
+            first = 64 + 32 * q + DRAFT_ROW
+            nc.scalar.dma_start(draft_plane[first : first + 4, :].bitcast(I32).rearrange("p (h n) -> p h n", h=2), draft_rows[q])
+        draft_codes = held.tile([P, T], I32, align_bytes=64)
+        nc.sync.dma_start(draft_codes[:], draft_words[0].rearrange("p n t -> p (n t)").bitcast(I32))
+
+        lists = []
+        for name, source in (("idx", offs), ("idx2", offs2), ("idx3", offs3), ("idx4", offs4), ("idx5", offs5)):
+            listed = held.tile([P, LIST_COLS], U16, name=name)
+            nc.sync.dma_start(listed[:], source)
+            lists.append(listed)
+        idx, idx2, idx3, idx4, idx5 = lists
+        lo_list, hi_list = slice(0, LIST_COLS // 2), slice(LIST_COLS // 2, LIST_COLS)
+        lo, hi = slice(0, HALF), slice(HALF, SLOTS)
+
+        f1 = held.tile([P, T], F32)
+        f2 = held.tile([P, T], F32)
+        nc.vector.memset(f1[:], 0.0)
+        nc.vector.memset(f2[:], 0.0)
+
+        q_grouped = held.tile([P, Q, PACK], BF16, align_bytes=64)
+        nc.vector.tensor_copy(q_grouped[:].rearrange("p (c i) t -> p c t i", i=4), q_raw[:].rearrange("p t (c i) -> p c t i", i=4))
+        nc.vector.tensor_copy(cache_plane[64:128, 0:T].bitcast(I32), cache_plane[0:64, T : 2 * T].bitcast(I32))
+        q_codes = held.tile([P, Q], U32, align_bytes=64)
+        q_plane = held.tile([P, Q], U8, align_bytes=64)
+        nc.vector.quantize_mx(out=q_codes[:].bitcast(FP8X4), scales=q_plane[:], in_=q_grouped[:].rearrange("p w j -> p (w j)"))
+        nc.vector.tensor_copy(draft_plane[0:64, T : 2 * T].bitcast(I32), draft_plane[64:128, 0:T].bitcast(I32))
+
+        a = held.tile([P, T], F32)
+        b = held.tile([P, T], F32)
+        for c in range(T // CHUNK):
+            bank = psum.tile([P, CHUNK], F32, name="a_bank%d" % c)
+            cols = slice(c * CHUNK, (c + 1) * CHUNK)
+            nc.tensor.matmul_mx(out=bank[:], lhsT=q_codes[:].bitcast(FP8X4), lhsT_scale=q_plane[:],
+                                rhs=cache_codes[:, 2 * c * CHUNK : 2 * (c + 1) * CHUNK].bitcast(FP4X4), rhs_scale=cache_plane[:, cols],
+                                start=True, stop=True)
+            if c % 2 == 0:
+                nc.scalar.activation(a[:, cols], bank[:], COPY)
+            else:
+                nc.vector.tensor_copy(a[:, cols], bank[:])
+        for c in range(T // CHUNK):
+            bank = psum.tile([P, CHUNK], F32, name="b_bank%d" % c)
+            cols = slice(c * CHUNK, (c + 1) * CHUNK)
+            nc.tensor.matmul_mx(out=bank[:], lhsT=q_codes[:].bitcast(FP8X4), lhsT_scale=q_plane[:],
+                                rhs=draft_codes[:, cols].bitcast(FP8X4),
+                                rhs_scale=draft_plane[DRAFT_ROW:P, T + c * CHUNK : T + (c + 1) * CHUNK],
+                                start=True, stop=True)
+            nc.scalar.activation(b[:, cols], bank[:], COPY)
+
+        a_picked = held.tile([P, SLOTS], F32)
+        nc.vector.tensor_scalar(a_picked[:], a[:].indirect(idx[:]), 1.0 / SLOTS, 0.0, ALU.mult, ALU.add)
+        b_picked = held.tile([P, SLOTS], F32)
+        nc.vector.tensor_copy(b_picked[:, lo], b[:].indirect(idx2[:, lo_list]))
+        nc.scalar.activation(b_picked[:, hi], b[:].indirect(idx2[:, hi_list]), COPY)
+
+        w_share = held.tile([P, SLOTS], F32)
+        mu = held.tile([P, 1], F32)
+        nc.vector.scalar_tensor_tensor(w_share[:], b_picked[:], 1.0 / SLOTS, a_picked[:], ALU.mult, ALU.max, accum_out=mu[:])
+        v = held.tile([P, SLOTS], F32)
+        nc.vector.tensor_scalar(v[:], w_share[:], float(SLOTS), mu[:], ALU.mult, ALU.subtract)
+
+        nc.scalar.activation(f1[:].indirect(idx3[:]), v[:], COPY)
+        nc.scalar.activation(f2[:].indirect(idx4[:]), v[:], COPY)
+
+        bb = held.tile([P, T], F32)
+        nc.vector.tensor_tensor(bb[:], b[:], f1[:], ALU.subtract)
+        bb_picked = held.tile([P, SLOTS], F32)
+        nc.vector.tensor_copy(bb_picked[:], bb[:].indirect(idx5[:]))
+
+        aa = held.tile([P, T], F32)
+        nc.vector.tensor_tensor(aa[:], a[:], f2[:], ALU.add)
+        r = held.tile([P, SLOTS], F32)
+        aa_picked = held.tile([P, HALF], F32)
+        nc.vector.tensor_tensor(r[:, lo], aa[:].indirect(idx[:, lo_list]), bb_picked[:, lo], ALU.add)
+        nc.scalar.activation(aa_picked[:], aa[:].indirect(idx[:, hi_list]), COPY)
+        nc.vector.tensor_tensor(r[:, hi], aa_picked[:], bb_picked[:, hi], ALU.add)
+        y = held.tile([P, SLOTS], F32)
+        for half in (lo, hi):
+            nc.vector.scalar_tensor_tensor(y[:, half], w_share[:, half], float(SLOTS), r[:, half], ALU.mult, ALU.min)
+            nc.sync.dma_start(out[:, half], y[:, half])

@@ -31,25 +31,22 @@ def tile_attend_centredwrites_two_kernel(tc, query, cache_words, cache_scales, d
         held = ctx.enter_context(tc.tile_pool(name="held", bufs=1))
         psum = ctx.enter_context(tc.psum_pool(name="psum", bufs=1))
 
-        cache_plane = held.tile([P, 2 * T], U8, align_bytes=64)
-        draft_plane = held.tile([P, 2 * T], U8, align_bytes=64)
-        nc.vector.memset(cache_plane[0:64, :].bitcast(I32), 0)
-        nc.vector.memset(draft_plane[64:128, :].bitcast(I32), 0)
+        cache_plane = held.tile([P, T], U8, align_bytes=64)
+        draft_plane = held.tile([P, T], U8, align_bytes=64)
+        nc.vector.memset(cache_plane[:].bitcast(I32), 0)
+        nc.vector.memset(draft_plane[:].bitcast(I32), 0)
 
         q_raw = held.tile([P, PACK, Q], F32)
         nc.sync.dma_start(q_raw[:], query.rearrange("(p j) w -> p j w", j=PACK))
-
-        cache_rows = cache_scales[0].bitcast(I32).rearrange("(h q k) n -> q k h n", h=2, q=2)
-        draft_rows = draft_scales[0].bitcast(I32).rearrange("(h q k) n -> q k h n", h=2, q=2)
-        for q in range(2):
-            nc.scalar.dma_start(cache_plane[32 * q : 32 * q + 4, :].bitcast(I32).rearrange("p (h n) -> p h n", h=2), cache_rows[q])
         cache_codes = held.tile([P, 2 * T], U8, align_bytes=64)
         nc.sync.dma_start(cache_codes[:].bitcast(I32), cache_words[0].bitcast(I32))
-        for q in range(2):
-            first = 64 + 32 * q + DRAFT_ROW
-            nc.scalar.dma_start(draft_plane[first : first + 4, :].bitcast(I32).rearrange("p (h n) -> p h n", h=2), draft_rows[q])
+        for g in range(4):
+            nc.sync.dma_start(cache_plane[32 * g : 32 * g + 4, :].bitcast(I32), cache_scales[0, 4 * g : 4 * g + 4, :].bitcast(I32))
         draft_codes = held.tile([P, T], I32, align_bytes=64)
         nc.sync.dma_start(draft_codes[:], draft_words[0].rearrange("p n t -> p (n t)").bitcast(I32))
+        for g in range(4):
+            first = 32 * g + DRAFT_ROW
+            nc.sync.dma_start(draft_plane[first : first + 4, :].bitcast(I32), draft_scales[0, 4 * g : 4 * g + 4, :].bitcast(I32))
 
         lists = []
         for name, source in (("idx", offs), ("idx2", offs2), ("idx3", offs3), ("idx4", offs4), ("idx5", offs5)):
@@ -64,14 +61,14 @@ def tile_attend_centredwrites_two_kernel(tc, query, cache_words, cache_scales, d
         f2 = held.tile([P, T], F32)
         nc.vector.memset(f1[:], 0.0)
         nc.vector.memset(f2[:], 0.0)
+        share = held.tile([P, 1], F32)
+        nc.vector.memset(share[:], 1.0 / SLOTS)
 
         q_grouped = held.tile([P, Q, PACK], BF16, align_bytes=64)
         nc.vector.tensor_copy(q_grouped[:].rearrange("p (c i) t -> p c t i", i=4), q_raw[:].rearrange("p t (c i) -> p c t i", i=4))
-        nc.vector.tensor_copy(cache_plane[64:128, 0:T].bitcast(I32), cache_plane[0:64, T : 2 * T].bitcast(I32))
         q_codes = held.tile([P, Q], U32, align_bytes=64)
         q_plane = held.tile([P, Q], U8, align_bytes=64)
         nc.vector.quantize_mx(out=q_codes[:].bitcast(FP8X4), scales=q_plane[:], in_=q_grouped[:].rearrange("p w j -> p (w j)"))
-        nc.vector.tensor_copy(draft_plane[0:64, T : 2 * T].bitcast(I32), draft_plane[64:128, 0:T].bitcast(I32))
 
         a = held.tile([P, T], F32)
         b = held.tile([P, T], F32)
@@ -90,38 +87,39 @@ def tile_attend_centredwrites_two_kernel(tc, query, cache_words, cache_scales, d
             cols = slice(c * CHUNK, (c + 1) * CHUNK)
             nc.tensor.matmul_mx(out=bank[:], lhsT=q_codes[:].bitcast(FP8X4), lhsT_scale=q_plane[:],
                                 rhs=draft_codes[:, cols].bitcast(FP8X4),
-                                rhs_scale=draft_plane[DRAFT_ROW:P, T + c * CHUNK : T + (c + 1) * CHUNK],
+                                rhs_scale=draft_plane[DRAFT_ROW:P, cols],
                                 start=True, stop=True)
             nc.scalar.activation(b[:, cols], bank[:], COPY)
 
         a_picked = held.tile([P, SLOTS], F32)
-        nc.vector.tensor_scalar(a_picked[:], a[:].indirect(idx[:]), 1.0 / SLOTS, 0.0, ALU.mult, ALU.add)
+        nc.vector.tensor_copy(a_picked[:], a[:].indirect(idx[:]))
         b_picked = held.tile([P, SLOTS], F32)
-        nc.vector.tensor_copy(b_picked[:, lo], b[:].indirect(idx2[:, lo_list]))
-        nc.scalar.activation(b_picked[:, hi], b[:].indirect(idx2[:, hi_list]), COPY)
+        nc.vector.tensor_scalar(b_picked[:, lo], b[:].indirect(idx2[:, lo_list]), 1.0 / SLOTS, 0.0, ALU.mult, ALU.add)
+        nc.scalar.activation(b_picked[:, hi], b[:].indirect(idx2[:, hi_list]), COPY, scale=share[:])
 
         w_share = held.tile([P, SLOTS], F32)
         mu = held.tile([P, 1], F32)
-        nc.vector.scalar_tensor_tensor(w_share[:], b_picked[:], 1.0 / SLOTS, a_picked[:], ALU.mult, ALU.max, accum_out=mu[:])
+        nc.vector.scalar_tensor_tensor(w_share[:], a_picked[:], 1.0 / SLOTS, b_picked[:], ALU.mult, ALU.max, accum_out=mu[:])
         v = held.tile([P, SLOTS], F32)
         nc.vector.tensor_scalar(v[:], w_share[:], float(SLOTS), mu[:], ALU.mult, ALU.subtract)
 
         nc.scalar.activation(f1[:].indirect(idx3[:]), v[:], COPY)
         nc.scalar.activation(f2[:].indirect(idx4[:]), v[:], COPY)
 
-        bb = held.tile([P, T], F32)
+        bb = held.tile([P, T], F32, tag="updated")
         nc.vector.tensor_tensor(bb[:], b[:], f1[:], ALU.subtract)
         bb_picked = held.tile([P, SLOTS], F32)
         nc.vector.tensor_copy(bb_picked[:], bb[:].indirect(idx5[:]))
 
-        aa = held.tile([P, T], F32)
+        aa = held.tile([P, T], F32, tag="updated")
         nc.vector.tensor_tensor(aa[:], a[:], f2[:], ALU.add)
         r = held.tile([P, SLOTS], F32)
         aa_picked = held.tile([P, HALF], F32)
         nc.vector.tensor_tensor(r[:, lo], aa[:].indirect(idx[:, lo_list]), bb_picked[:, lo], ALU.add)
         nc.scalar.activation(aa_picked[:], aa[:].indirect(idx[:, hi_list]), COPY)
         nc.vector.tensor_tensor(r[:, hi], aa_picked[:], bb_picked[:, hi], ALU.add)
-        y = held.tile([P, SLOTS], F32)
-        for half in (lo, hi):
-            nc.vector.scalar_tensor_tensor(y[:, half], w_share[:, half], float(SLOTS), r[:, half], ALU.mult, ALU.min)
-            nc.sync.dma_start(out[:, half], y[:, half])
+        y_lo = held.tile([P, HALF], F32, tag="updated")
+        y_hi = held.tile([P, HALF], F32)
+        for half, y in ((lo, y_lo), (hi, y_hi)):
+            nc.vector.scalar_tensor_tensor(y[:], w_share[:, half], float(SLOTS), r[:, half], ALU.mult, ALU.min)
+            nc.sync.dma_start(out[:, half], y[:])

@@ -19,6 +19,8 @@ PACK = 4
 CHUNK = 256
 HALF = SLOTS // 2
 LIST_COLS = SLOTS // 16
+LEAD = 64
+VECTOR_RUNS = 22
 DRAFT_ROW = 4
 
 FLOPS = 2 * D * Q * 2 * T
@@ -65,7 +67,10 @@ def tile_attend_centredwrites_two_kernel(tc, query, cache_words, cache_scales, d
         nc.vector.memset(share[:], 1.0 / SLOTS)
 
         q_grouped = held.tile([P, Q, PACK], BF16, align_bytes=64)
-        nc.vector.tensor_copy(q_grouped[:].rearrange("p (c i) t -> p c t i", i=4), q_raw[:].rearrange("p t (c i) -> p c t i", i=4))
+        q_to = q_grouped[:].rearrange("p (c i) t -> p c t i", i=4)
+        q_from = q_raw[:].rearrange("p t (c i) -> p c t i", i=4)
+        nc.vector.tensor_copy(q_to[:, 0:VECTOR_RUNS], q_from[:, 0:VECTOR_RUNS])
+        nc.scalar.activation(q_to[:, VECTOR_RUNS : Q // 4], q_from[:, VECTOR_RUNS : Q // 4], COPY)
         q_codes = held.tile([P, Q], U32, align_bytes=64)
         q_plane = held.tile([P, Q], U8, align_bytes=64)
         nc.vector.quantize_mx(out=q_codes[:].bitcast(FP8X4), scales=q_plane[:], in_=q_grouped[:].rearrange("p w j -> p (w j)"))
@@ -101,10 +106,12 @@ def tile_attend_centredwrites_two_kernel(tc, query, cache_words, cache_scales, d
         mu = held.tile([P, 1], F32)
         nc.vector.scalar_tensor_tensor(w_share[:], a_picked[:], 1.0 / SLOTS, b_picked[:], ALU.mult, ALU.max, accum_out=mu[:])
         v = held.tile([P, SLOTS], F32)
-        nc.vector.tensor_scalar(v[:], w_share[:], float(SLOTS), mu[:], ALU.mult, ALU.subtract)
+        for part in (slice(0, LEAD), slice(LEAD, SLOTS)):
+            nc.vector.tensor_scalar(v[:, part], w_share[:, part], float(SLOTS), mu[:], ALU.mult, ALU.subtract)
 
+        nc.scalar.activation(f2[:].indirect(idx4[:, 0 : LEAD // 16]), v[:, 0:LEAD], COPY)
         nc.scalar.activation(f1[:].indirect(idx3[:]), v[:], COPY)
-        nc.scalar.activation(f2[:].indirect(idx4[:]), v[:], COPY)
+        nc.scalar.activation(f2[:].indirect(idx4[:, LEAD // 16 : LIST_COLS]), v[:, LEAD:SLOTS], COPY)
 
         bb = held.tile([P, T], F32, tag="updated")
         nc.vector.tensor_tensor(bb[:], b[:], f1[:], ALU.subtract)

from contextlib import ExitStack

import concourse.mybir as mybir

F32 = mybir.dt.float32
BF16 = mybir.dt.bfloat16
I32 = mybir.dt.int32
U32 = mybir.dt.uint32
U16 = mybir.dt.uint16
U8 = mybir.dt.uint8
FP8X4 = mybir.dt.float8_e4m3fn_x4
FP4X4 = mybir.dt.float4_e2m1fn_x4
ALU = mybir.AluOpType
COPY = mybir.ActivationFunctionType.Copy

P = 128
D, T, SLOTS, Q = 512, 1024, 512, 128
PACK = 4
CHUNK = 256
HALF = SLOTS // 2
LIST_COLS = SLOTS // 16
LEAD = 64
VECTOR_RUNS = 22
DRAFT_ROW = 4

FLOPS = 2 * D * Q * 2 * T


def tile_attend_centredwrites_two_kernel(tc, query, cache_words, cache_scales, draft_words, draft_scales,
                                          offs, offs2, offs3, offs4, offs5, out):
    nc = tc.nc
    with ExitStack() as ctx:
        held = ctx.enter_context(tc.tile_pool(name="held", bufs=1))
        psum = ctx.enter_context(tc.psum_pool(name="psum", bufs=1))

        cache_plane = held.tile([P, T], U8, align_bytes=64)
        draft_plane = held.tile([P, T], U8, align_bytes=64)
        nc.vector.memset(cache_plane[:].bitcast(I32), 0)
        nc.vector.memset(draft_plane[:].bitcast(I32), 0)

        q_raw = held.tile([P, PACK, Q], F32)
        nc.sync.dma_start(q_raw[:], query.rearrange("(p j) w -> p j w", j=PACK))
        cache_codes = held.tile([P, 2 * T], U8, align_bytes=64)
        nc.sync.dma_start(cache_codes[:].bitcast(I32), cache_words[0].bitcast(I32))
        for g in range(4):
            nc.sync.dma_start(cache_plane[32 * g : 32 * g + 4, :].bitcast(I32), cache_scales[0, 4 * g : 4 * g + 4, :].bitcast(I32))
        draft_codes = held.tile([P, T], I32, align_bytes=64)
        nc.sync.dma_start(draft_codes[:], draft_words[0].rearrange("p n t -> p (n t)").bitcast(I32))
        for g in range(4):
            first = 32 * g + DRAFT_ROW
            nc.sync.dma_start(draft_plane[first : first + 4, :].bitcast(I32), draft_scales[0, 4 * g : 4 * g + 4, :].bitcast(I32))

        lists = []
        for name, source in (("idx", offs), ("idx2", offs2), ("idx3", offs3), ("idx4", offs4), ("idx5", offs5)):
            listed = held.tile([P, LIST_COLS], U16, name=name)
            nc.sync.dma_start(listed[:], source)
            lists.append(listed)
        idx, idx2, idx3, idx4, idx5 = lists
        lo_list, hi_list = slice(0, LIST_COLS // 2), slice(LIST_COLS // 2, LIST_COLS)
        lo, hi = slice(0, HALF), slice(HALF, SLOTS)

        f1 = held.tile([P, T], F32)
        f2 = held.tile([P, T], F32)
        nc.vector.memset(f1[:], 0.0)
        nc.vector.memset(f2[:], 0.0)
        share = held.tile([P, 1], F32)
        nc.vector.memset(share[:], 1.0 / SLOTS)

        q_grouped = held.tile([P, Q, PACK], BF16, align_bytes=64)
        q_to = q_grouped[:].rearrange("p (c i) t -> p c t i", i=4)
        q_from = q_raw[:].rearrange("p t (c i) -> p c t i", i=4)
        nc.vector.tensor_copy(q_to[:, 0:VECTOR_RUNS], q_from[:, 0:VECTOR_RUNS])
        nc.scalar.activation(q_to[:, VECTOR_RUNS : Q // 4], q_from[:, VECTOR_RUNS : Q // 4], COPY)
        q_codes = held.tile([P, Q], U32, align_bytes=64)
        q_plane = held.tile([P, Q], U8, align_bytes=64)
        nc.vector.quantize_mx(out=q_codes[:].bitcast(FP8X4), scales=q_plane[:], in_=q_grouped[:].rearrange("p w j -> p (w j)"))

        a = held.tile([P, T], F32)
        b = held.tile([P, T], F32)
        for c in range(T // CHUNK):
            bank = psum.tile([P, CHUNK], F32, name="a_bank%d" % c)
            cols = slice(c * CHUNK, (c + 1) * CHUNK)
            nc.tensor.matmul_mx(out=bank[:], lhsT=q_codes[:].bitcast(FP8X4), lhsT_scale=q_plane[:],
                                rhs=cache_codes[:, 2 * c * CHUNK : 2 * (c + 1) * CHUNK].bitcast(FP4X4), rhs_scale=cache_plane[:, cols],
                                start=True, stop=True)
            if c % 2 == 0:
                nc.scalar.activation(a[:, cols], bank[:], COPY)
            else:
                nc.vector.tensor_copy(a[:, cols], bank[:])
        for c in range(T // CHUNK):
            bank = psum.tile([P, CHUNK], F32, name="b_bank%d" % c)
            cols = slice(c * CHUNK, (c + 1) * CHUNK)
            nc.tensor.matmul_mx(out=bank[:], lhsT=q_codes[:].bitcast(FP8X4), lhsT_scale=q_plane[:],
                                rhs=draft_codes[:, cols].bitcast(FP8X4),
                                rhs_scale=draft_plane[DRAFT_ROW:P, cols],
                                start=True, stop=True)
            nc.scalar.activation(b[:, cols], bank[:], COPY)

        a_picked = held.tile([P, SLOTS], F32)
        nc.vector.tensor_copy(a_picked[:], a[:].indirect(idx[:]))
        b_picked = held.tile([P, SLOTS], F32)
        nc.vector.tensor_scalar(b_picked[:, lo], b[:].indirect(idx2[:, lo_list]), 1.0 / SLOTS, 0.0, ALU.mult, ALU.add)
        nc.scalar.activation(b_picked[:, hi], b[:].indirect(idx2[:, hi_list]), COPY, scale=share[:])

        w_share = held.tile([P, SLOTS], F32)
        mu = held.tile([P, 1], F32)
        nc.vector.scalar_tensor_tensor(w_share[:], a_picked[:], 1.0 / SLOTS, b_picked[:], ALU.mult, ALU.max, accum_out=mu[:])
        v = held.tile([P, SLOTS], F32)
        for part in (slice(0, LEAD), slice(LEAD, SLOTS)):
            nc.vector.tensor_scalar(v[:, part], w_share[:, part], float(SLOTS), mu[:], ALU.mult, ALU.subtract)

        nc.scalar.activation(f2[:].indirect(idx4[:, 0 : LEAD // 16]), v[:, 0:LEAD], COPY)
        nc.scalar.activation(f1[:].indirect(idx3[:]), v[:], COPY)
        nc.scalar.activation(f2[:].indirect(idx4[:, LEAD // 16 : LIST_COLS]), v[:, LEAD:SLOTS], COPY)

        bb = held.tile([P, T], F32, tag="updated")
        nc.vector.tensor_tensor(bb[:], b[:], f1[:], ALU.subtract)
        bb_picked = held.tile([P, SLOTS], F32)
        nc.vector.tensor_copy(bb_picked[:], bb[:].indirect(idx5[:]))

        aa = held.tile([P, T], F32, tag="updated")
        nc.vector.tensor_tensor(aa[:], a[:], f2[:], ALU.add)
        r = held.tile([P, SLOTS], F32)
        aa_picked = held.tile([P, HALF], F32)
        nc.vector.tensor_tensor(r[:, lo], aa[:].indirect(idx[:, lo_list]), bb_picked[:, lo], ALU.add)
        nc.scalar.activation(aa_picked[:], aa[:].indirect(idx[:, hi_list]), COPY)
        nc.vector.tensor_tensor(r[:, hi], aa_picked[:], bb_picked[:, hi], ALU.add)
        y_lo = held.tile([P, HALF], F32, tag="updated")
        y_hi = held.tile([P, HALF], F32)
        for half, y in ((lo, y_lo), (hi, y_hi)):
            nc.vector.scalar_tensor_tensor(y[:], w_share[:, half], float(SLOTS), r[:, half], ALU.mult, ALU.min)
            nc.sync.dma_start(out[:, half], y[:])
